import numpy as np
import ml_dtypes


def mxq(x, axis, fmt="e4m3"):
    dtype, down = {"e4m3": (ml_dtypes.float8_e4m3fn, 7), "e5m2": (ml_dtypes.float8_e5m2, 14)}[fmt]
    v = np.moveaxis(np.asarray(x, np.float32).astype(ml_dtypes.bfloat16).astype(np.float64), axis, -1)
    blocks = v.reshape(v.shape[:-1] + (-1, 32))
    amax = np.abs(blocks).max(-1, keepdims=True)
    byte = np.maximum(np.where(amax > 0, np.frexp(amax)[1] - 1 + 127, 0) - down, 1)
    scale = np.exp2(byte - 127.0)
    codes = (blocks / scale).astype(np.float32).astype(dtype).astype(np.float64)
    return np.moveaxis((codes * scale).reshape(v.shape), -1, axis)


WIDE = False


def mx_kscale(k):
    if not WIDE:
        return np.ones(k)
    levels = np.array([30, -30])
    if k % 512:
        return np.exp2(np.random.permutation(np.resize(levels, k // 32))).repeat(32)
    a = np.empty((k // 512, 16))
    for p in range(k // 512):
        a[p, :8] = np.random.permutation(np.resize(levels, 8))
        for g in range(8):
            far = levels[np.abs(levels - a[p, g]) >= 10]
            a[p, g + 8] = far[np.random.randint(len(far))]
    return np.exp2(a.ravel()).repeat(32)


def f64(x):
    return np.asarray(x).astype(np.float64)


def striped(idx):
    return np.tile(np.asarray(idx).reshape(-1, 16).T, (8, 1)).astype(np.uint16)


def unstriped(offs):
    return offs[:16].T.reshape(-1).astype(np.int64)


E2M1 = np.array([0.0, 0.5, 1.0, 1.5, 2.0, 3.0, 4.0, 6.0, -0.0, -0.5, -1.0, -1.5, -2.0, -3.0, -4.0, -6.0])


def pack_weight(w, fmt):
    k, n = w.shape
    w = f64(np.asarray(w, np.float32).astype(ml_dtypes.bfloat16)).reshape(k // 32, 32, n)
    amax = np.abs(w).max(1)
    if fmt in ("e4m3", "e5m2"):
        byte = np.frexp(amax)[1] - 1 + 127 - (7 if fmt == "e4m3" else 14)
    else:
        mant, ex = np.frexp(amax / 6.0)
        byte = np.where(mant > 0.5, ex, ex - 1) + 127
    byte = np.clip(np.where(amax > 0, byte, 1), 1, 254)
    scaled = (w * np.exp2(127.0 - byte)[:, None, :]).reshape(k, n).astype(np.float32)
    by_word = np.ascontiguousarray(scaled.reshape(k // 512, 128, 4, n).transpose(0, 1, 3, 2))
    if fmt in ("e4m3", "e5m2"):
        words = by_word.astype(ml_dtypes.float8_e4m3fn if fmt == "e4m3" else ml_dtypes.float8_e5m2).view(np.uint8)
    else:
        c = by_word.astype(ml_dtypes.float4_e2m1fn).view(np.uint8) & 0xF
        words = (c[..., 0::2] | (c[..., 1::2] << 4)).reshape(k // 512, 128, 2 * n)
    return np.ascontiguousarray(words), np.ascontiguousarray(byte.astype(np.uint8).reshape(k // 512, 16, n))


def unpack_weight(words, scales, fmt):
    g, _, n = scales.shape
    words = np.ascontiguousarray(words).reshape(g, 128, n, -1)
    if fmt in ("e4m3", "e5m2"):
        vals = words.view(ml_dtypes.float8_e4m3fn if fmt == "e4m3" else ml_dtypes.float8_e5m2).astype(np.float64)
    else:
        nib = np.empty((g, 128, n, 4), np.uint8)
        nib[..., 0::2] = words & 0xF
        nib[..., 1::2] = words >> 4
        vals = E2M1[nib]
    vals = vals * np.repeat(np.exp2(scales.astype(np.float64) - 127.0), 8, axis=1)[..., None]
    return vals.transpose(0, 1, 3, 2).reshape(g * 512, n)


K, T, J, I, L, S, R, C, O, N = 1024, 1024, 256, 128, 128, 512, 512, 1024, 256, 256


def setup_inputs():
    n = np.random.standard_normal
    idx = np.random.permutation(T)[:I]
    idx2 = np.random.permutation(S)[:L]
    idx3 = np.random.permutation(C)[:J]
    idx4 = np.random.permutation(C)[:O]
    fk = mx_kscale(K)
    fr = mx_kscale(R)
    wp = pack_weight(n((K, R)) * 1 / np.sqrt(K) * fk[:, None] * fr, "e5m2")
    wbp = pack_weight(n((R, N)) * 1 / np.sqrt(R) / fr[:, None], "e2m1")
    return {
        "xa": (n((K, T)) / fk[:, None]).astype(np.float32),
        "xb": (n((K, S)) * 0.6 / fk[:, None]).astype(np.float32),
        "w_words": wp[0],
        "w_scales": wp[1],
        "oldh": (n((R, C)) * 0.7 * fr[:, None]).astype(np.float32),
        "wb_words": wbp[0],
        "wb_scales": wbp[1],
        "rs": (1.0 * n((O, N))).astype(np.float32),
        "offs": striped(idx),
        "offs2": striped(idx2),
        "offs3": striped(idx3),
        "offs4": striped(idx4),
    }


def reference(xa, xb, w_words, w_scales, oldh, wb_words, wb_scales, rs, offs, offs2, offs3, offs4):
    idx = unstriped(offs)
    idx2 = unstriped(offs2)
    idx3 = unstriped(offs3)
    idx4 = unstriped(offs4)
    wu = unpack_weight(w_words, w_scales, "e5m2")
    wbu = unpack_weight(wb_words, wb_scales, "e2m1")
    u = np.concatenate([f64(xa)[:, idx], f64(xb)[:, idx2]], axis=1)
    uq = mxq(u, 0, "e5m2")
    a = wu.T @ uq
    ha = np.maximum(a, 0.0)
    pw0 = np.zeros((R, C))
    pw0[:, idx3] = ha
    pg = pw0 + f64(oldh)
    hid = pg[:, idx4]
    hidq = mxq(hid, 0, "e5m2")
    p = hidq.T @ wbu
    mn = np.mean(np.abs(p), axis=1, keepdims=True)
    y = np.maximum(p - mn, 0.0) - 0.3 * f64(rs)
    return y

@@ -1,0 +1,185 @@
+from contextlib import ExitStack
+
+import concourse.mybir as mybir
+
+K, T, J, S, R, C, O, N = 1024, 1024, 256, 512, 512, 1024, 256, 256
+FLOPS = 2 * K * R * J + 2 * R * O * N
+
+F32 = mybir.dt.float32
+BF16 = mybir.dt.bfloat16
+I32 = mybir.dt.int32
+U32 = mybir.dt.uint32
+U16 = mybir.dt.uint16
+U8 = mybir.dt.uint8
+E5M2 = mybir.dt.float8_e5m2_x4
+E2M1 = mybir.dt.float4_e2m1fn_x4
+ALU = mybir.AluOpType
+ACT = mybir.ActivationFunctionType
+
+P = 128
+PACK = 4
+KP = P * PACK
+H = 128
+
+
+def tile_list_page_joined_rowabove_kernel(
+    tc, xa, xb, w_words, w_scales, oldh, wb_words, wb_scales, rs, offs, offs2, offs3, offs4, out
+):
+    nc = tc.nc
+    with ExitStack() as ctx:
+        lists = ctx.enter_context(tc.tile_pool(name="lists", bufs=1))
+        sb = ctx.enter_context(tc.tile_pool(name="sb", bufs=1))
+        ps = ctx.enter_context(tc.psum_pool(name="ps", bufs=1))
+
+        la = lists.tile([P, 8], U16, name="la")
+        lb = lists.tile([P, 8], U16, name="lb")
+        lput = lists.tile([P, 16], U16, name="lput")
+        lget = lists.tile([P, 16], U16, name="lget")
+
+        w_raw = sb.tile([P, 2, R], U32, name="w_raw", align_bytes=64)
+        ws_raw = sb.tile([P, 2, R], U8, name="ws_raw", align_bytes=64)
+        w_q = sb.tile([P, 2, PACK, H], U32, name="w_q", align_bytes=64)
+        ws_q = sb.tile([P, 2, PACK, H], U8, name="ws_q", align_bytes=64)
+        wb_q = sb.tile([P, 2 * N], U8, name="wb_q", align_bytes=64)
+        wbs_q = sb.tile([P, N], U8, name="wbs_q", align_bytes=64)
+        xb_t = [sb.tile([P, PACK, S], F32, name=f"xb{z}") for z in range(2)]
+        xa_runs = [(0, 0, 4), (1, 0, 2), (1, 2, 1), (1, 3, 1)]
+        xa_t = [sb.tile([P, n, T], F32, name=f"xa{i}") for i, (z, t0, n) in enumerate(xa_runs)]
+        old_t = [sb.tile([P, C], F32, name=f"old{t}") for t in range(PACK)]
+        put_t = [sb.tile([P, C], F32, name=f"put{t}") for t in range(PACK)]
+        pg_t = [sb.tile([P, C], F32, name=f"pg{t}") for t in range(PACK)]
+        rs_t = sb.tile([P, 2, N], F32, name="rs_t")
+
+        nc.gpsimd.memset(ws_raw[:].rearrange("p z c -> p (z c)").bitcast(I32), 0)
+        nc.gpsimd.memset(wbs_q[:].bitcast(I32), 0)
+        for t in range(PACK):
+            nc.vector.memset(put_t[t][:], 0.0)
+
+        xa_v = xa.rearrange("(z p t) c -> z p t c", p=P, t=PACK)
+        xb_v = xb.rearrange("(z p t) c -> z p t c", p=P, t=PACK)
+        old_v = oldh.rearrange("(p t) c -> p t c", t=PACK)
+
+        nc.sync.dma_start(out=w_raw[:].bitcast(I32), in_=w_words.rearrange("z p c r -> p z (c r)").bitcast(I32))
+        for q in range(4):
+            nc.sync.dma_start(
+                out=ws_raw[32 * q : 32 * q + 4, :, :].bitcast(I32),
+                in_=w_scales[:, 4 * q : 4 * q + 4, :].rearrange("z r c -> r z c").bitcast(I32),
+            )
+        nc.sync.dma_start(out=xb_t[0][:], in_=xb_v[0])
+        nc.sync.dma_start(lb[:], offs2)
+        nc.sync.dma_start(out=xb_t[1][:], in_=xb_v[1])
+        nc.sync.dma_start(lput[:], offs3)
+        nc.sync.dma_start(la[:], offs)
+        for i, (z, t0, n) in enumerate(xa_runs):
+            nc.sync.dma_start(out=xa_t[i][:], in_=xa_v[z, :, t0 : t0 + n, :])
+        nc.sync.dma_start(lget[:], offs4)
+        for t in range(PACK):
+            nc.sync.dma_start(out=old_t[t][:], in_=old_v[:, t, :])
+        nc.sync.dma_start(out=wb_q[:].bitcast(I32), in_=wb_words[0].bitcast(I32))
+        for q in range(4):
+            nc.sync.dma_start(
+                out=wbs_q[32 * q : 32 * q + 4, :].bitcast(I32),
+                in_=wb_scales[0, 4 * q : 4 * q + 4, :].bitcast(I32),
+            )
+        nc.sync.dma_start(out=rs_t[:], in_=rs.rearrange("(h p) n -> p h n", p=P))
+
+        nc.vector.tensor_copy(
+            out=w_q[:].rearrange("p z t m -> p z m t"), in_=w_raw[:].rearrange("p z (m t) -> p z m t", t=PACK)
+        )
+        nc.vector.tensor_copy(
+            out=ws_q[:].rearrange("p z t m -> p z m t"), in_=ws_raw[:].rearrange("p z (m t) -> p z m t", t=PACK)
+        )
+
+        def first_product(acc, z, t, codes, scales):
+            nc.tensor.matmul_mx(
+                out=acc,
+                lhsT=w_q[:, z, t, :].bitcast(E5M2),
+                lhsT_scale=ws_q[:, z, t, :],
+                rhs=codes.bitcast(E5M2),
+                rhs_scale=scales,
+                start=(z == 0),
+                stop=(z == 1),
+            )
+
+        ub = sb.tile([P, 2, H, PACK], BF16, name="ub", align_bytes=64)
+        ub_c = sb.tile([P, 2, H], U32, name="ub_c", align_bytes=64)
+        ub_s = sb.tile([P, 2, H], U8, name="ub_s", align_bytes=64)
+        for z in range(2):
+            for t in range(PACK):
+                nc.vector.tensor_copy(out=ub[:, z, :, t], in_=xb_t[z][:, t, :].indirect(lb[:]))
+        nc.vector.quantize_mx(
+            out=ub_c[:].rearrange("p z j -> p (z j)").bitcast(E5M2),
+            scales=ub_s[:].rearrange("p z j -> p (z j)"),
+            in_=ub[:].rearrange("p z j t -> p (z j t)"),
+        )
+        acc_b = ps.tile([P, PACK, H], F32, name="acc_b")
+        for t in range(PACK):
+            for z in range(2):
+                first_product(acc_b[:, t, :], z, t, ub_c[:, z, :], ub_s[:, z, :])
+        hb = sb.tile([P, PACK, H], F32, name="hb")
+        nc.scalar.activation(out=hb[:], in_=acc_b[:], func=ACT.Relu)
+        for t in range(PACK):
+            nc.scalar.activation(out=put_t[t][:].indirect(lput[:, 8:16]), in_=hb[:, t, :], func=ACT.Copy)
+
+        ua = [sb.tile([P, H, PACK], BF16, name=f"ua{z}", align_bytes=64) for z in range(2)]
+        ua_c = [sb.tile([P, H], U32, name=f"ua_c{z}", align_bytes=64) for z in range(2)]
+        ua_s = [sb.tile([P, H], U8, name=f"ua_s{z}", align_bytes=64) for z in range(2)]
+        acc_a = [ps.tile([P, H], F32, name=f"acc_a{t}") for t in range(PACK)]
+        for z in range(2):
+            for i, (zz, t0, n) in enumerate(xa_runs):
+                if zz == z:
+                    for t in range(n):
+                        nc.vector.tensor_copy(out=ua[z][:, :, t0 + t], in_=xa_t[i][:, t, :].indirect(la[:]))
+            nc.vector.quantize_mx(
+                out=ua_c[z][:].bitcast(E5M2), scales=ua_s[z][:], in_=ua[z][:].rearrange("p j t -> p (j t)")
+            )
+            for t in range(PACK):
+                first_product(acc_a[t][:], z, t, ua_c[z][:], ua_s[z][:])
+        ha = [sb.tile([P, H], F32, name=f"ha{t}") for t in range(PACK)]
+        for t in range(PACK):
+            nc.vector.tensor_scalar_max(out=ha[t][:], in0=acc_a[t][:], scalar1=0.0)
+        for t in range(PACK):
+            nc.scalar.activation(out=put_t[t][:].indirect(lput[:, 0:8]), in_=ha[t][:], func=ACT.Copy)
+
+        got = sb.tile([P, PACK, O], BF16, name="got")
+        for t in range(PACK):
+            nc.vector.tensor_tensor(out=pg_t[t][:], in0=put_t[t][:], in1=old_t[t][:], op=ALU.add)
+            if t < PACK - 1:
+                nc.scalar.activation(out=got[:, t, :], in_=pg_t[t][:].indirect(lget[:]), func=ACT.Copy)
+            else:
+                nc.vector.tensor_copy(out=got[:, t, 0:H], in_=pg_t[t][:].indirect(lget[:, 0:8]))
+                nc.scalar.activation(out=got[:, t, H:O], in_=pg_t[t][:].indirect(lget[:, 8:16]), func=ACT.Copy)
+
+        hq = [sb.tile([P, H, PACK], BF16, name=f"hq{h}", align_bytes=64) for h in range(2)]
+        hq_c = [sb.tile([P, H], U32, name=f"hq_c{h}", align_bytes=64) for h in range(2)]
+        hq_s = [sb.tile([P, H], U8, name=f"hq_s{h}", align_bytes=64) for h in range(2)]
+        acc_p = [ps.tile([P, N], F32, name=f"acc_p{h}") for h in range(2)]
+        mag = [sb.tile([P, N], F32, name=f"mag{h}") for h in range(2)]
+        mean = [sb.tile([P, 1], F32, name=f"mean{h}") for h in range(2)]
+        above = [sb.tile([P, N], F32, name=f"above{h}") for h in range(2)]
+        res = [sb.tile([P, N], F32, name=f"res{h}") for h in range(2)]
+        for h in range(2):
+            nc.vector.tensor_copy(out=hq[h][:], in_=got[:, :, h * H : (h + 1) * H].rearrange("p t o -> p o t"))
+        for h in range(2):
+            nc.vector.quantize_mx(
+                out=hq_c[h][:].bitcast(E5M2), scales=hq_s[h][:], in_=hq[h][:].rearrange("p o t -> p (o t)")
+            )
+            nc.tensor.matmul_mx(
+                out=acc_p[h][:],
+                lhsT=hq_c[h][:].bitcast(E5M2),
+                lhsT_scale=hq_s[h][:],
+                rhs=wb_q[:].bitcast(E2M1),
+                rhs_scale=wbs_q[:],
+                start=True,
+                stop=True,
+            )
+            nc.scalar.activation(out=mag[h][:], in_=acc_p[h][:], func=ACT.Abs, scale=1.0 / N, accum_out=mean[h][:])
+        for h in range(2):
+            nc.vector.tensor_scalar(
+                out=above[h][:], in0=acc_p[h][:], scalar1=mean[h][:], scalar2=0.0, op0=ALU.subtract, op1=ALU.max
+            )
+        for h in range(2):
+            nc.vector.scalar_tensor_tensor(
+                out=res[h][:], in0=rs_t[:, h, :], scalar=-0.3, in1=above[h][:], op0=ALU.mult, op1=ALU.add
+            )
+            nc.sync.dma_start(out=out[h * H : (h + 1) * H, :], in_=res[h][:])

@@ -43,7 +43,7 @@ def tile_list_page_joined_rowabove_kernel(
         wb_q = sb.tile([P, 2 * N], U8, name="wb_q", align_bytes=64)
         wbs_q = sb.tile([P, N], U8, name="wbs_q", align_bytes=64)
         xb_t = [sb.tile([P, PACK, S], F32, name=f"xb{z}") for z in range(2)]
-        xa_runs = [(0, 0, 4), (1, 0, 2), (1, 2, 1), (1, 3, 1)]
+        xa_runs = [(0, 0, 2), (0, 2, 2), (1, 0, 2), (1, 2, 1), (1, 3, 1)]
         xa_t = [sb.tile([P, n, T], F32, name=f"xa{i}") for i, (z, t0, n) in enumerate(xa_runs)]
         old_t = [sb.tile([P, C], F32, name=f"old{t}") for t in range(PACK)]
         put_t = [sb.tile([P, C], F32, name=f"put{t}") for t in range(PACK)]
@@ -139,7 +139,10 @@ def tile_list_page_joined_rowabove_kernel(
         for t in range(PACK):
             nc.vector.tensor_scalar_max(out=ha[t][:], in0=acc_a[t][:], scalar1=0.0)
         for t in range(PACK):
-            nc.scalar.activation(out=put_t[t][:].indirect(lput[:, 0:8]), in_=ha[t][:], func=ACT.Copy)
+            if t == 1:
+                nc.vector.tensor_copy(out=put_t[t][:].indirect(lput[:, 0:8]), in_=ha[t][:])
+            else:
+                nc.scalar.activation(out=put_t[t][:].indirect(lput[:, 0:8]), in_=ha[t][:], func=ACT.Copy)
 
         got = sb.tile([P, PACK, O], BF16, name="got")
         for t in range(PACK):
@@ -159,7 +162,12 @@ def tile_list_page_joined_rowabove_kernel(
         above = [sb.tile([P, N], F32, name=f"above{h}") for h in range(2)]
         res = [sb.tile([P, N], F32, name=f"res{h}") for h in range(2)]
         for h in range(2):
-            nc.vector.tensor_copy(out=hq[h][:], in_=got[:, :, h * H : (h + 1) * H].rearrange("p t o -> p o t"))
+            src = got[:, :, h * H : (h + 1) * H].rearrange("p t (c i) -> p c t i", i=4)
+            dst = hq[h][:].rearrange("p (c i) t -> p c t i", i=4)
+            if h == 0:
+                nc.vector.tensor_copy(out=dst, in_=src)
+            else:
+                nc.scalar.copy(out=dst, in_=src)
         for h in range(2):
             nc.vector.quantize_mx(
                 out=hq_c[h][:].bitcast(E5M2), scales=hq_s[h][:], in_=hq[h][:].rearrange("p o t -> p (o t)")
@@ -174,12 +182,12 @@ def tile_list_page_joined_rowabove_kernel(
                 stop=True,
             )
             nc.scalar.activation(out=mag[h][:], in_=acc_p[h][:], func=ACT.Abs, scale=1.0 / N, accum_out=mean[h][:])
-        for h in range(2):
-            nc.vector.tensor_scalar(
-                out=above[h][:], in0=acc_p[h][:], scalar1=mean[h][:], scalar2=0.0, op0=ALU.subtract, op1=ALU.max
-            )
+        nc.vector.tensor_scalar(
+            out=above[0][:], in0=rs_t[:, 0, :], scalar1=0.3, scalar2=mean[0][:], op0=ALU.mult, op1=ALU.add
+        )
+        nc.scalar.activation(out=above[1][:], in_=rs_t[:, 1, :], func=ACT.Identity, scale=0.3, bias=mean[1][:])
         for h in range(2):
             nc.vector.scalar_tensor_tensor(
-                out=res[h][:], in0=rs_t[:, h, :], scalar=-0.3, in1=above[h][:], op0=ALU.mult, op1=ALU.add
+                out=res[h][:], in0=acc_p[h][:], scalar=mean[h][:], in1=above[h][:], op0=ALU.max, op1=ALU.subtract
             )
             nc.sync.dma_start(out=out[h * H : (h + 1) * H, :], in_=res[h][:])

@@ -60,18 +60,19 @@ def tile_list_page_joined_rowabove_kernel(
         old_v = oldh.rearrange("(p t) c -> p t c", t=PACK)
 
         nc.sync.dma_start(out=w_raw[:].bitcast(I32), in_=w_words.rearrange("z p c r -> p z (c r)").bitcast(I32))
+        nc.sync.dma_start(out=xb_t[0][:], in_=xb_v[0])
+        nc.sync.dma_start(lb[:], offs2)
         for q in range(4):
             nc.sync.dma_start(
                 out=ws_raw[32 * q : 32 * q + 4, :, :].bitcast(I32),
                 in_=w_scales[:, 4 * q : 4 * q + 4, :].rearrange("z r c -> r z c").bitcast(I32),
             )
-        nc.sync.dma_start(out=xb_t[0][:], in_=xb_v[0])
-        nc.sync.dma_start(lb[:], offs2)
         nc.sync.dma_start(out=xb_t[1][:], in_=xb_v[1])
-        nc.sync.dma_start(lput[:], offs3)
         nc.sync.dma_start(la[:], offs)
         for i, (z, t0, n) in enumerate(xa_runs):
             nc.sync.dma_start(out=xa_t[i][:], in_=xa_v[z, :, t0 : t0 + n, :])
+            if i == 0:
+                nc.sync.dma_start(lput[:], offs3)
         nc.sync.dma_start(lget[:], offs4)
         for t in range(PACK):
             nc.sync.dma_start(out=old_t[t][:], in_=old_v[:, t, :])

@@ -40,6 +40,8 @@ def tile_list_page_joined_rowabove_kernel(
         ws_raw = sb.tile([P, 2, R], U8, name="ws_raw", align_bytes=64)
         w_q = sb.tile([P, 2, PACK, H], U32, name="w_q", align_bytes=64)
         ws_q = sb.tile([P, 2, PACK, H], U8, name="ws_q", align_bytes=64)
+        wb_raw = sb.tile([P, 2 * N], U8, name="wb_raw")
+        wbs_raw = sb.tile([P, N], U8, name="wbs_raw")
         wb_q = sb.tile([P, 2 * N], U8, name="wb_q", align_bytes=64)
         wbs_q = sb.tile([P, N], U8, name="wbs_q", align_bytes=64)
         xb_t = [sb.tile([P, PACK, S], F32, name=f"xb{z}") for z in range(2)]
@@ -51,7 +53,7 @@ def tile_list_page_joined_rowabove_kernel(
         rs_t = sb.tile([P, 2, N], F32, name="rs_t")
 
         nc.gpsimd.memset(ws_raw[:].rearrange("p z c -> p (z c)").bitcast(I32), 0)
-        nc.gpsimd.memset(wbs_q[:].bitcast(I32), 0)
+        nc.gpsimd.memset(wbs_raw[:].bitcast(I32), 0)
         for t in range(PACK):
             nc.vector.memset(put_t[t][:], 0.0)
 
@@ -73,16 +75,16 @@ def tile_list_page_joined_rowabove_kernel(
             nc.sync.dma_start(out=xa_t[i][:], in_=xa_v[z, :, t0 : t0 + n, :])
             if i == 0:
                 nc.sync.dma_start(lput[:], offs3)
+        nc.sync.dma_start(out=wb_raw[:].bitcast(I32), in_=wb_words[0].bitcast(I32))
         nc.sync.dma_start(lget[:], offs4)
-        for t in range(PACK):
-            nc.sync.dma_start(out=old_t[t][:], in_=old_v[:, t, :])
-        nc.sync.dma_start(out=wb_q[:].bitcast(I32), in_=wb_words[0].bitcast(I32))
+        nc.sync.dma_start(out=rs_t[:], in_=rs.rearrange("(h p) n -> p h n", p=P))
         for q in range(4):
             nc.sync.dma_start(
-                out=wbs_q[32 * q : 32 * q + 4, :].bitcast(I32),
+                out=wbs_raw[32 * q : 32 * q + 4, :].bitcast(I32),
                 in_=wb_scales[0, 4 * q : 4 * q + 4, :].bitcast(I32),
             )
-        nc.sync.dma_start(out=rs_t[:], in_=rs.rearrange("(h p) n -> p h n", p=P))
+        for t in range(PACK):
+            nc.sync.dma_start(out=old_t[t][:], in_=old_v[:, t, :])
 
         nc.vector.tensor_copy(
             out=w_q[:].rearrange("p z t m -> p z m t"), in_=w_raw[:].rearrange("p z (m t) -> p z m t", t=PACK)
@@ -136,6 +138,8 @@ def tile_list_page_joined_rowabove_kernel(
             )
             for t in range(PACK):
                 first_product(acc_a[t][:], z, t, ua_c[z][:], ua_s[z][:])
+        nc.vector.tensor_copy(out=wb_q[:].bitcast(I32), in_=wb_raw[:].bitcast(I32))
+        nc.vector.tensor_copy(out=wbs_q[:].bitcast(I32), in_=wbs_raw[:].bitcast(I32))
         ha = [sb.tile([P, H], F32, name=f"ha{t}") for t in range(PACK)]
         for t in range(PACK):
             nc.vector.tensor_scalar_max(out=ha[t][:], in0=acc_a[t][:], scalar1=0.0)
@@ -183,10 +187,10 @@ def tile_list_page_joined_rowabove_kernel(
                 stop=True,
             )
             nc.scalar.activation(out=mag[h][:], in_=acc_p[h][:], func=ACT.Abs, scale=1.0 / N, accum_out=mean[h][:])
-        nc.vector.tensor_scalar(
-            out=above[0][:], in0=rs_t[:, 0, :], scalar1=0.3, scalar2=mean[0][:], op0=ALU.mult, op1=ALU.add
-        )
-        nc.scalar.activation(out=above[1][:], in_=rs_t[:, 1, :], func=ACT.Identity, scale=0.3, bias=mean[1][:])
+        for h in range(2):
+            nc.vector.tensor_scalar(
+                out=above[h][:], in0=rs_t[:, h, :], scalar1=0.3, scalar2=mean[h][:], op0=ALU.mult, op1=ALU.add
+            )
         for h in range(2):
             nc.vector.scalar_tensor_tensor(
                 out=res[h][:], in0=acc_p[h][:], scalar=mean[h][:], in1=above[h][:], op0=ALU.max, op1=ALU.subtract

from contextlib import ExitStack

import concourse.mybir as mybir

K, T, J, S, R, C, O, N = 1024, 1024, 256, 512, 512, 1024, 256, 256
FLOPS = 2 * K * R * J + 2 * R * O * N

F32 = mybir.dt.float32
BF16 = mybir.dt.bfloat16
I32 = mybir.dt.int32
U32 = mybir.dt.uint32
U16 = mybir.dt.uint16
U8 = mybir.dt.uint8
E5M2 = mybir.dt.float8_e5m2_x4
E2M1 = mybir.dt.float4_e2m1fn_x4
ALU = mybir.AluOpType
ACT = mybir.ActivationFunctionType

P = 128
PACK = 4
KP = P * PACK
H = 128


def tile_list_page_joined_rowabove_kernel(
    tc, xa, xb, w_words, w_scales, oldh, wb_words, wb_scales, rs, offs, offs2, offs3, offs4, out
):
    nc = tc.nc
    with ExitStack() as ctx:
        lists = ctx.enter_context(tc.tile_pool(name="lists", bufs=1))
        sb = ctx.enter_context(tc.tile_pool(name="sb", bufs=1))
        ps = ctx.enter_context(tc.psum_pool(name="ps", bufs=1))

        la = lists.tile([P, 8], U16, name="la")
        lb = lists.tile([P, 8], U16, name="lb")
        lput = lists.tile([P, 16], U16, name="lput")
        lget = lists.tile([P, 16], U16, name="lget")

        w_raw = sb.tile([P, 2, R], U32, name="w_raw", align_bytes=64)
        ws_raw = sb.tile([P, 2, R], U8, name="ws_raw", align_bytes=64)
        w_q = sb.tile([P, 2, PACK, H], U32, name="w_q", align_bytes=64)
        ws_q = sb.tile([P, 2, PACK, H], U8, name="ws_q", align_bytes=64)
        wb_raw = sb.tile([P, 2 * N], U8, name="wb_raw")
        wbs_raw = sb.tile([P, N], U8, name="wbs_raw")
        wb_q = sb.tile([P, 2 * N], U8, name="wb_q", align_bytes=64)
        wbs_q = sb.tile([P, N], U8, name="wbs_q", align_bytes=64)
        xb_t = [sb.tile([P, PACK, S], F32, name=f"xb{z}") for z in range(2)]
        xa_runs = [(0, 0, 2), (0, 2, 2), (1, 0, 2), (1, 2, 1), (1, 3, 1)]
        xa_t = [sb.tile([P, n, T], F32, name=f"xa{i}") for i, (z, t0, n) in enumerate(xa_runs)]
        old_t = [sb.tile([P, C], F32, name=f"old{t}") for t in range(PACK)]
        put_t = [sb.tile([P, C], F32, name=f"put{t}") for t in range(PACK)]
        pg_t = [sb.tile([P, C], F32, name=f"pg{t}") for t in range(PACK)]
        rs_t = sb.tile([P, 2, N], F32, name="rs_t")

        nc.gpsimd.memset(ws_raw[:].rearrange("p z c -> p (z c)").bitcast(I32), 0)
        nc.gpsimd.memset(wbs_raw[:].bitcast(I32), 0)
        for t in range(PACK):
            nc.vector.memset(put_t[t][:], 0.0)

        xa_v = xa.rearrange("(z p t) c -> z p t c", p=P, t=PACK)
        xb_v = xb.rearrange("(z p t) c -> z p t c", p=P, t=PACK)
        old_v = oldh.rearrange("(p t) c -> p t c", t=PACK)

        nc.sync.dma_start(out=w_raw[:].bitcast(I32), in_=w_words.rearrange("z p c r -> p z (c r)").bitcast(I32))
        nc.sync.dma_start(out=xb_t[0][:], in_=xb_v[0])
        nc.sync.dma_start(lb[:], offs2)
        for q in range(4):
            nc.sync.dma_start(
                out=ws_raw[32 * q : 32 * q + 4, :, :].bitcast(I32),
                in_=w_scales[:, 4 * q : 4 * q + 4, :].rearrange("z r c -> r z c").bitcast(I32),
            )
        nc.sync.dma_start(out=xb_t[1][:], in_=xb_v[1])
        nc.sync.dma_start(la[:], offs)
        for i, (z, t0, n) in enumerate(xa_runs):
            nc.sync.dma_start(out=xa_t[i][:], in_=xa_v[z, :, t0 : t0 + n, :])
            if i == 0:
                nc.sync.dma_start(lput[:], offs3)
        nc.sync.dma_start(out=wb_raw[:].bitcast(I32), in_=wb_words[0].bitcast(I32))
        nc.sync.dma_start(lget[:], offs4)
        nc.sync.dma_start(out=rs_t[:], in_=rs.rearrange("(h p) n -> p h n", p=P))
        for q in range(4):
            nc.sync.dma_start(
                out=wbs_raw[32 * q : 32 * q + 4, :].bitcast(I32),
                in_=wb_scales[0, 4 * q : 4 * q + 4, :].bitcast(I32),
            )
        for t in range(PACK):
            nc.sync.dma_start(out=old_t[t][:], in_=old_v[:, t, :])

        nc.vector.tensor_copy(
            out=w_q[:].rearrange("p z t m -> p z m t"), in_=w_raw[:].rearrange("p z (m t) -> p z m t", t=PACK)
        )
        nc.vector.tensor_copy(
            out=ws_q[:].rearrange("p z t m -> p z m t"), in_=ws_raw[:].rearrange("p z (m t) -> p z m t", t=PACK)
        )

        def first_product(acc, z, t, codes, scales):
            nc.tensor.matmul_mx(
                out=acc,
                lhsT=w_q[:, z, t, :].bitcast(E5M2),
                lhsT_scale=ws_q[:, z, t, :],
                rhs=codes.bitcast(E5M2),
                rhs_scale=scales,
                start=(z == 0),
                stop=(z == 1),
            )

        ub = sb.tile([P, 2, H, PACK], BF16, name="ub", align_bytes=64)
        ub_c = sb.tile([P, 2, H], U32, name="ub_c", align_bytes=64)
        ub_s = sb.tile([P, 2, H], U8, name="ub_s", align_bytes=64)
        for z in range(2):
            for t in range(PACK):
                nc.vector.tensor_copy(out=ub[:, z, :, t], in_=xb_t[z][:, t, :].indirect(lb[:]))
        nc.vector.quantize_mx(
            out=ub_c[:].rearrange("p z j -> p (z j)").bitcast(E5M2),
            scales=ub_s[:].rearrange("p z j -> p (z j)"),
            in_=ub[:].rearrange("p z j t -> p (z j t)"),
        )
        acc_b = ps.tile([P, PACK, H], F32, name="acc_b")
        for t in range(PACK):
            for z in range(2):
                first_product(acc_b[:, t, :], z, t, ub_c[:, z, :], ub_s[:, z, :])
        hb = sb.tile([P, PACK, H], F32, name="hb")
        nc.scalar.activation(out=hb[:], in_=acc_b[:], func=ACT.Relu)
        for t in range(PACK):
            nc.scalar.activation(out=put_t[t][:].indirect(lput[:, 8:16]), in_=hb[:, t, :], func=ACT.Copy)

        ua = [sb.tile([P, H, PACK], BF16, name=f"ua{z}", align_bytes=64) for z in range(2)]
        ua_c = [sb.tile([P, H], U32, name=f"ua_c{z}", align_bytes=64) for z in range(2)]
        ua_s = [sb.tile([P, H], U8, name=f"ua_s{z}", align_bytes=64) for z in range(2)]
        acc_a = [ps.tile([P, H], F32, name=f"acc_a{t}") for t in range(PACK)]
        for z in range(2):
            for i, (zz, t0, n) in enumerate(xa_runs):
                if zz == z:
                    for t in range(n):
                        nc.vector.tensor_copy(out=ua[z][:, :, t0 + t], in_=xa_t[i][:, t, :].indirect(la[:]))
            nc.vector.quantize_mx(
                out=ua_c[z][:].bitcast(E5M2), scales=ua_s[z][:], in_=ua[z][:].rearrange("p j t -> p (j t)")
            )
            for t in range(PACK):
                first_product(acc_a[t][:], z, t, ua_c[z][:], ua_s[z][:])
        nc.vector.tensor_copy(out=wb_q[:].bitcast(I32), in_=wb_raw[:].bitcast(I32))
        nc.vector.tensor_copy(out=wbs_q[:].bitcast(I32), in_=wbs_raw[:].bitcast(I32))
        ha = [sb.tile([P, H], F32, name=f"ha{t}") for t in range(PACK)]
        for t in range(PACK):
            nc.vector.tensor_scalar_max(out=ha[t][:], in0=acc_a[t][:], scalar1=0.0)
        for t in range(PACK):
            if t == 1:
                nc.vector.tensor_copy(out=put_t[t][:].indirect(lput[:, 0:8]), in_=ha[t][:])
            else:
                nc.scalar.activation(out=put_t[t][:].indirect(lput[:, 0:8]), in_=ha[t][:], func=ACT.Copy)

        got = sb.tile([P, PACK, O], BF16, name="got")
        for t in range(PACK):
            nc.vector.tensor_tensor(out=pg_t[t][:], in0=put_t[t][:], in1=old_t[t][:], op=ALU.add)
            if t < PACK - 1:
                nc.scalar.activation(out=got[:, t, :], in_=pg_t[t][:].indirect(lget[:]), func=ACT.Copy)
            else:
                nc.vector.tensor_copy(out=got[:, t, 0:H], in_=pg_t[t][:].indirect(lget[:, 0:8]))
                nc.scalar.activation(out=got[:, t, H:O], in_=pg_t[t][:].indirect(lget[:, 8:16]), func=ACT.Copy)

        hq = [sb.tile([P, H, PACK], BF16, name=f"hq{h}", align_bytes=64) for h in range(2)]
        hq_c = [sb.tile([P, H], U32, name=f"hq_c{h}", align_bytes=64) for h in range(2)]
        hq_s = [sb.tile([P, H], U8, name=f"hq_s{h}", align_bytes=64) for h in range(2)]
        acc_p = [ps.tile([P, N], F32, name=f"acc_p{h}") for h in range(2)]
        mag = [sb.tile([P, N], F32, name=f"mag{h}") for h in range(2)]
        mean = [sb.tile([P, 1], F32, name=f"mean{h}") for h in range(2)]
        above = [sb.tile([P, N], F32, name=f"above{h}") for h in range(2)]
        res = [sb.tile([P, N], F32, name=f"res{h}") for h in range(2)]
        for h in range(2):
            src = got[:, :, h * H : (h + 1) * H].rearrange("p t (c i) -> p c t i", i=4)
            dst = hq[h][:].rearrange("p (c i) t -> p c t i", i=4)
            if h == 0:
                nc.vector.tensor_copy(out=dst, in_=src)
            else:
                nc.scalar.copy(out=dst, in_=src)
        for h in range(2):
            nc.vector.quantize_mx(
                out=hq_c[h][:].bitcast(E5M2), scales=hq_s[h][:], in_=hq[h][:].rearrange("p o t -> p (o t)")
            )
            nc.tensor.matmul_mx(
                out=acc_p[h][:],
                lhsT=hq_c[h][:].bitcast(E5M2),
                lhsT_scale=hq_s[h][:],
                rhs=wb_q[:].bitcast(E2M1),
                rhs_scale=wbs_q[:],
                start=True,
                stop=True,
            )
            nc.scalar.activation(out=mag[h][:], in_=acc_p[h][:], func=ACT.Abs, scale=1.0 / N, accum_out=mean[h][:])
        for h in range(2):
            nc.vector.tensor_scalar(
                out=above[h][:], in0=rs_t[:, h, :], scalar1=0.3, scalar2=mean[h][:], op0=ALU.mult, op1=ALU.add
            )
        for h in range(2):
            nc.vector.scalar_tensor_tensor(
                out=res[h][:], in0=acc_p[h][:], scalar=mean[h][:], in1=above[h][:], op0=ALU.max, op1=ALU.subtract
            )
            nc.sync.dma_start(out=out[h * H : (h + 1) * H, :], in_=res[h][:])
